import numpy as np
import ml_dtypes


def mxq(x, axis, fmt="e4m3"):
    dtype, down = {"e4m3": (ml_dtypes.float8_e4m3fn, 7), "e5m2": (ml_dtypes.float8_e5m2, 14)}[fmt]
    v = np.moveaxis(np.asarray(x, np.float32).astype(ml_dtypes.bfloat16).astype(np.float64), axis, -1)
    blocks = v.reshape(v.shape[:-1] + (-1, 32))
    amax = np.abs(blocks).max(-1, keepdims=True)
    byte = np.maximum(np.where(amax > 0, np.frexp(amax)[1] - 1 + 127, 0) - down, 1)
    scale = np.exp2(byte - 127.0)
    codes = (blocks / scale).astype(np.float32).astype(dtype).astype(np.float64)
    return np.moveaxis((codes * scale).reshape(v.shape), -1, axis)


WIDE = False


def mx_kscale(k):
    if not WIDE:
        return np.ones(k)
    levels = np.array([10, -10, 5, -5, 0])
    if k % 512:
        return np.exp2(np.random.permutation(np.resize(levels, k // 32))).repeat(32)
    a = np.empty((k // 512, 16))
    for p in range(k // 512):
        a[p, :8] = np.random.permutation(np.resize(levels, 8))
        for g in range(8):
            far = levels[np.abs(levels - a[p, g]) >= 10]
            a[p, g + 8] = far[np.random.randint(len(far))]
    return np.exp2(a.ravel()).repeat(32)


def f64(x):
    return np.asarray(x).astype(np.float64)


def striped(idx):
    return np.tile(np.asarray(idx).reshape(-1, 16).T, (8, 1)).astype(np.uint16)


def unstriped(offs):
    return offs[:16].T.reshape(-1).astype(np.int64)


E2M1 = np.array([0.0, 0.5, 1.0, 1.5, 2.0, 3.0, 4.0, 6.0, -0.0, -0.5, -1.0, -1.5, -2.0, -3.0, -4.0, -6.0])


def pack_weight(w, fmt):
    k, n = w.shape
    w = f64(np.asarray(w, np.float32).astype(ml_dtypes.bfloat16)).reshape(k // 32, 32, n)
    amax = np.abs(w).max(1)
    if fmt == "e4m3":
        byte = np.frexp(amax)[1] - 1 + 127 - 7
    else:
        mant, ex = np.frexp(amax / 6.0)
        byte = np.where(mant > 0.5, ex, ex - 1) + 127
    byte = np.clip(np.where(amax > 0, byte, 1), 1, 254)
    scaled = (w * np.exp2(127.0 - byte)[:, None, :]).reshape(k, n).astype(np.float32)
    by_word = np.ascontiguousarray(scaled.reshape(k // 512, 128, 4, n).transpose(0, 1, 3, 2))
    if fmt == "e4m3":
        words = by_word.astype(ml_dtypes.float8_e4m3fn).view(np.uint8)
    else:
        c = by_word.astype(ml_dtypes.float4_e2m1fn).view(np.uint8) & 0xF
        words = (c[..., 0::2] | (c[..., 1::2] << 4)).reshape(k // 512, 128, 2 * n)
    return np.ascontiguousarray(words), np.ascontiguousarray(byte.astype(np.uint8).reshape(k // 512, 16, n))


def unpack_weight(words, scales, fmt):
    g, _, n = scales.shape
    words = np.ascontiguousarray(words).reshape(g, 128, n, -1)
    if fmt == "e4m3":
        vals = words.view(ml_dtypes.float8_e4m3fn).astype(np.float64)
    else:
        nib = np.empty((g, 128, n, 4), np.uint8)
        nib[..., 0::2] = words & 0xF
        nib[..., 1::2] = words >> 4
        vals = E2M1[nib]
    vals = vals * np.repeat(np.exp2(scales.astype(np.float64) - 127.0), 8, axis=1)[..., None]
    return vals.transpose(0, 1, 3, 2).reshape(g * 512, n)


def sigmoid(v):
    return 1.0 / (1.0 + np.exp(-v))


D, E, T, I, Q = 512, 512, 2048, 512, 128


def setup_inputs():
    n = np.random.standard_normal
    idx = np.random.permutation(T)[:I]
    fd = mx_kscale(D)
    fi = mx_kscale(I)
    ti = np.ones(T)
    ti[idx] = fi
    keysp = pack_weight(n((D, T)) / fd[:, None], "e2m1")
    return {
        "query": (n((D, Q)) * 0.8 / np.sqrt(D) * fd[:, None]).astype(np.float32),
        "keys_words": keysp[0],
        "keys_scales": keysp[1],
        "share": (np.random.uniform(0.2, 0.8, (Q, 1))).astype(np.float32),
        "dquery": (n((D, Q)) * 0.6 / np.sqrt(D) * fd[:, None]).astype(np.float32),
        "os": (np.random.uniform(4.0, 16.0, (1, I)) * fi).astype(np.float32),
        "vals": (n((E, T)) / ti).astype(np.float32),
        "offs": striped(idx),
    }


def reference(query, keys_words, keys_scales, share, dquery, os, vals, offs):
    idx = unstriped(offs)
    keysu = unpack_weight(keys_words, keys_scales, "e2m1")
    queryq = mxq(f64(query), 0, "e4m3")
    keysidxg = keysu[:, idx]
    a = queryq.T @ keysidxg
    dqueryq = mxq(f64(dquery), 0, "e4m3")
    ta = dqueryq.T @ keysidxg
    e0 = np.exp(a)
    s0 = sigmoid(a)
    p = e0 * f64(share) + s0 * (1.0 - f64(share)) * 3.0
    z = np.sum(p, axis=1, keepdims=True)
    te0 = ta * e0
    ts0 = ta * s0 * (1.0 - s0)
    tp = te0 * f64(share) + ts0 * (1.0 - f64(share)) * 3.0
    tz = np.sum(tp, axis=1, keepdims=True)
    tw = (tp - tz * p / z) / z
    wo1 = tw * f64(os)
    wt1 = wo1.T
    vt1 = f64(vals)[:, idx].T
    wt1q = mxq(wt1, 0, "e4m3")
    vt1q = mxq(vt1, 0, "e4m3")
    o = wt1q.T @ vt1q
    return o

@@ -1,0 +1,183 @@
+from contextlib import ExitStack
+
+import concourse.mybir as mybir
+from concourse.masks import make_identity
+
+D, E, T, I, Q = 512, 512, 2048, 512, 128
+FLOPS = 2 * (2 * Q * D * I + Q * I * E)
+
+F32 = mybir.dt.float32
+BF16 = mybir.dt.bfloat16
+I32 = mybir.dt.int32
+U32 = mybir.dt.uint32
+U16 = mybir.dt.uint16
+U8 = mybir.dt.uint8
+FP8X4 = mybir.dt.float8_e4m3fn_x4
+FP4X4 = mybir.dt.float4_e2m1fn_x4
+ACT = mybir.ActivationFunctionType
+MULT = mybir.AluOpType.mult
+ADD = mybir.AluOpType.add
+
+P = 128
+PACK = 4
+E_TILES = E // P
+
+
+def tile_attend_ttmixedparts_kernel(tc, query, keys_words, keys_scales, share, dquery, slot_factor, vals, offs, out):
+    nc = tc.nc
+    with ExitStack() as ctx:
+        sb = ctx.enter_context(tc.tile_pool(name="sb", bufs=1))
+        ps = ctx.enter_context(tc.psum_pool(name="ps", bufs=1))
+        ps_turn = ctx.enter_context(tc.psum_pool(name="ps_turn", bufs=2))
+
+        offsets = sb.tile([P, I // 16], U16, name="offsets")
+        nc.sync.dma_start(offsets[:], offs)
+
+        key_scales = sb.tile([P, T], U8, name="key_scales", align_bytes=64)
+        nc.vector.memset(key_scales[:].bitcast(I32), 0)
+        key_words = sb.tile([P, T], U16, name="key_words", align_bytes=64)
+        nc.sync.dma_start(key_words[:].bitcast(I32), keys_words[0].bitcast(I32))
+        for quad in range(4):
+            nc.sync.dma_start(
+                key_scales[32 * quad : 32 * quad + 4, :].bitcast(I32),
+                keys_scales[0, 4 * quad : 4 * quad + 4, :].bitcast(I32),
+            )
+        raw_q = []
+        for name, src in (("q", query), ("dq", dquery)):
+            raw = sb.tile([P, PACK, Q], F32, name="raw_" + name)
+            nc.sync.dma_start(raw[:], src.rearrange("(p j) q -> p j q", j=PACK))
+            raw_q.append(raw)
+        pool_vals = [sb.tile([P, T], F32, name="vals%d" % j) for j in range(E_TILES)]
+        nc.sync.dma_start(pool_vals[0][:], vals[0:P, :])
+        share_col = sb.tile([P, 1], F32, name="share_col")
+        nc.sync.dma_start(share_col[:], share)
+        os_cols = sb.tile([P, PACK], F32, name="os_cols")
+        nc.sync.dma_start(os_cols[:], slot_factor.rearrange("o (p t) -> (o p) t", t=PACK))
+        for j in range(1, E_TILES):
+            nc.sync.dma_start(pool_vals[j][:], vals[j * P : (j + 1) * P, :])
+
+        warm = sb.tile([P, 1], F32, name="warm")
+        nc.gpsimd.memset(warm[:], 0.0)
+        warm_out = sb.tile([P, 1], F32, name="warm_out")
+        nc.scalar.activation(warm_out[:], warm[:], ACT.Sigmoid)
+
+        ident = sb.tile([P, P], F32, name="ident")
+        make_identity(nc, ident[:])
+
+        got_words = sb.tile([P, I], U16, name="got_words", align_bytes=64)
+        nc.vector.tensor_copy(got_words[:], key_words[:].indirect(offsets[:]))
+        got_scales = sb.tile([P, I], U8, name="got_scales", align_bytes=64)
+        nc.vector.tensor_copy(got_scales[:], key_scales[:].indirect(offsets[:]))
+
+        scores = []
+        for name, raw in zip(("q", "dq"), raw_q):
+            grouped = sb.tile([P, Q * PACK], BF16, name="grouped_" + name, align_bytes=64)
+            nc.scalar.copy(
+                grouped[:].rearrange("p (c i t) -> p c t i", i=4, t=PACK),
+                raw[:].rearrange("p t (c i) -> p c t i", i=4),
+            )
+            codes = sb.tile([P, Q], U32, name="codes_" + name, align_bytes=64)
+            scales = sb.tile([P, Q], U8, name="scales_" + name, align_bytes=64)
+            nc.vector.quantize_mx(out=codes[:].bitcast(FP8X4), scales=scales[:], in_=grouped[:])
+            acc = ps.tile([P, I], F32, name="score_" + name)
+            nc.tensor.matmul_mx(
+                out=acc[:], lhsT=codes[:].bitcast(FP8X4), lhsT_scale=scales[:],
+                rhs=got_words[:].bitcast(FP4X4), rhs_scale=got_scales[:], start=True, stop=True,
+            )
+            scores.append(acc)
+        a, ta = scores
+
+        coef = sb.tile([P, 1], F32, name="coef")
+        nc.gpsimd.tensor_scalar(coef[:], share_col[:], -3.0, 3.0, MULT, ADD)
+
+        os_rows = ps.tile([P, PACK, P], F32, name="os_rows")
+        for t in range(PACK):
+            nc.tensor.transpose(os_rows[:, t, :], os_cols[:, t : t + 1].to_broadcast([P, P]), ident[:])
+
+        def turn(src, name):
+            words = src[:].bitcast(F32)
+            turned = ps_turn.tile([P, 2, P], F32, name="turned")
+            for u in range(2):
+                nc.tensor.transpose(turned[:, u, :], words[:, u : I // 2 : 2], ident[:])
+            grouped = sb.tile([P, P * PACK], BF16, name="grouped_" + name, align_bytes=64)
+            nc.scalar.copy(
+                grouped[:].bitcast(F32).rearrange("p (r u) -> p r u", u=2),
+                turned[:].rearrange("p u r -> p r u"),
+            )
+            return grouped
+
+        v_codes = sb.tile([P, E], U32, name="v_codes", align_bytes=64)
+        v_scales = sb.tile([P, E], U8, name="v_scales", align_bytes=64)
+
+        def gather_vals(j, tag):
+            got = sb.tile([P, I], BF16, name="got_vals%d" % j, tag=tag, align_bytes=64)
+            nc.vector.tensor_copy(got[:], pool_vals[j][:].indirect(offsets[:]))
+            return turn(got, "v%d" % j)
+
+        def quantize_vals(j, grouped):
+            cols = slice(j * P, (j + 1) * P)
+            nc.vector.quantize_mx(out=v_codes[:, cols].bitcast(FP8X4), scales=v_scales[:, cols], in_=grouped[:])
+
+        rest = sb.tile([P, I], F32, name="rest")
+        nc.scalar.activation(rest[:], a[:], ACT.Sigmoid, scale=-1.0)
+        e0 = sb.tile([P, I], F32, name="e0")
+        nc.scalar.activation(e0[:], a[:], ACT.Exp)
+        mix = sb.tile([P, I], F32, name="mix", tag="mix", align_bytes=64)
+        nc.scalar.activation(mix[:], rest[:], ACT.Identity, bias=share_col[:], scale=coef[:])
+
+        g0 = gather_vals(0, "first")
+        curv = sb.tile([P, I], F32, name="curv", tag="curv", align_bytes=64)
+        nc.vector.scalar_tensor_tensor(curv[:], rest[:], coef[:], rest[:], MULT, MULT)
+        slope = sb.tile([P, I], F32, name="slope")
+        nc.vector.scalar_tensor_tensor(slope[:], curv[:], share_col[:], ta[:], ADD, MULT)
+        g1 = gather_vals(1, "curv")
+        tp = sb.tile([P, I], F32, name="tp")
+        tz = sb.tile([P, 1], F32, name="tz")
+        nc.vector.scalar_tensor_tensor(tp[:], slope[:], 1.0, e0[:], MULT, MULT, accum_out=tz[:])
+        part = sb.tile([P, I], F32, name="part")
+        z = sb.tile([P, 1], F32, name="z")
+        nc.vector.scalar_tensor_tensor(part[:], mix[:], 1.0, e0[:], MULT, MULT, accum_out=z[:])
+        g2 = gather_vals(2, "mix")
+        rz = sb.tile([P, 1], F32, name="rz")
+        nc.vector.reciprocal(rz[:], z[:])
+        quantize_vals(0, g0)
+        neg_k = sb.tile([P, 1], F32, name="neg_k")
+        nc.vector.tensor_scalar(neg_k[:], tz[:], rz[:], -1.0, MULT, MULT)
+        centred = sb.tile([P, I], F32, name="centred", tag="centred", align_bytes=64)
+        nc.vector.scalar_tensor_tensor(centred[:], part[:], neg_k[:], tp[:], MULT, ADD)
+        quantize_vals(1, g1)
+        w = sb.tile([P, I], BF16, name="w", align_bytes=64)
+        nc.vector.scalar_tensor_tensor(
+            w[:].rearrange("q (p t) -> q p t", t=PACK),
+            centred[:].rearrange("q (p t) -> q p t", t=PACK),
+            rz[:],
+            os_rows[:].rearrange("q t p -> q p t"),
+            MULT, MULT,
+        )
+        gw = turn(w, "w")
+        g3 = gather_vals(3, "centred")
+        quantize_vals(2, g2)
+        w_codes = sb.tile([P, Q], U32, name="w_codes", align_bytes=64)
+        w_scales = sb.tile([P, Q], U8, name="w_scales", align_bytes=64)
+        nc.vector.quantize_mx(out=w_codes[:].bitcast(FP8X4), scales=w_scales[:], in_=gw[:])
+
+        def product(acc, at, cols):
+            n = cols.stop - cols.start
+            nc.tensor.matmul_mx(
+                out=acc[:, at : at + n], lhsT=w_codes[:].bitcast(FP8X4), lhsT_scale=w_scales[:],
+                rhs=v_codes[:, cols].bitcast(FP8X4), rhs_scale=v_scales[:, cols], start=True, stop=True,
+            )
+
+        early = ps.tile([P, 3 * P], F32, name="early")
+        product(early, 0, slice(0, 2 * P))
+        product(early, 2 * P, slice(2 * P, 3 * P))
+        early_sb = sb.tile([P, 3 * P], F32, name="early_sb")
+        nc.scalar.copy(early_sb[:], early[:])
+        nc.sync.dma_start(out[:, 0 : 3 * P], early_sb[:])
+
+        quantize_vals(3, g3)
+        late = ps.tile([P, P], F32, name="late")
+        product(late, 0, slice(3 * P, 4 * P))
+        late_sb = sb.tile([P, P], F32, name="late_sb")
+        nc.vector.tensor_copy(late_sb[:], late[:])
+        nc.sync.dma_start(out[:, 3 * P : 4 * P], late_sb[:])

@@ -28,33 +28,35 @@ def tile_attend_ttmixedparts_kernel(tc, query, keys_words, keys_scales, share, d
     with ExitStack() as ctx:
         sb = ctx.enter_context(tc.tile_pool(name="sb", bufs=1))
         ps = ctx.enter_context(tc.psum_pool(name="ps", bufs=1))
-        ps_turn = ctx.enter_context(tc.psum_pool(name="ps_turn", bufs=2))
+        ps_turn = ctx.enter_context(tc.psum_pool(name="ps_turn", bufs=1))
 
         offsets = sb.tile([P, I // 16], U16, name="offsets")
         nc.sync.dma_start(offsets[:], offs)
 
         key_scales = sb.tile([P, T], U8, name="key_scales", align_bytes=64)
-        nc.vector.memset(key_scales[:].bitcast(I32), 0)
-        key_words = sb.tile([P, T], U16, name="key_words", align_bytes=64)
-        nc.sync.dma_start(key_words[:].bitcast(I32), keys_words[0].bitcast(I32))
+        nc.gpsimd.memset(key_scales[:].bitcast(I32), 0)
         for quad in range(4):
             nc.sync.dma_start(
                 key_scales[32 * quad : 32 * quad + 4, :].bitcast(I32),
                 keys_scales[0, 4 * quad : 4 * quad + 4, :].bitcast(I32),
             )
+        key_words = sb.tile([P, T], U16, name="key_words", align_bytes=64)
+        nc.sync.dma_start(key_words[:].bitcast(I32), keys_words[0].bitcast(I32))
+        halves = [slice(0, T // 2), slice(T // 2, T)]
         raw_q = []
         for name, src in (("q", query), ("dq", dquery)):
             raw = sb.tile([P, PACK, Q], F32, name="raw_" + name)
             nc.sync.dma_start(raw[:], src.rearrange("(p j) q -> p j q", j=PACK))
             raw_q.append(raw)
-        pool_vals = [sb.tile([P, T], F32, name="vals%d" % j) for j in range(E_TILES)]
+        pool_vals = [sb.tile([P, T], F32, name="vals%d" % j, tag="vals%d" % j, align_bytes=64) for j in range(E_TILES)]
         nc.sync.dma_start(pool_vals[0][:], vals[0:P, :])
         share_col = sb.tile([P, 1], F32, name="share_col")
         nc.sync.dma_start(share_col[:], share)
         os_cols = sb.tile([P, PACK], F32, name="os_cols")
         nc.sync.dma_start(os_cols[:], slot_factor.rearrange("o (p t) -> (o p) t", t=PACK))
         for j in range(1, E_TILES):
-            nc.sync.dma_start(pool_vals[j][:], vals[j * P : (j + 1) * P, :])
+            for cols in (halves if j == 2 else [slice(0, T)]):
+                nc.sync.dma_start(pool_vals[j][:, cols], vals[j * P : (j + 1) * P, cols])
 
         warm = sb.tile([P, 1], F32, name="warm")
         nc.gpsimd.memset(warm[:], 0.0)
@@ -64,10 +66,11 @@ def tile_attend_ttmixedparts_kernel(tc, query, keys_words, keys_scales, share, d
         ident = sb.tile([P, P], F32, name="ident")
         make_identity(nc, ident[:])
 
-        got_words = sb.tile([P, I], U16, name="got_words", align_bytes=64)
-        nc.vector.tensor_copy(got_words[:], key_words[:].indirect(offsets[:]))
         got_scales = sb.tile([P, I], U8, name="got_scales", align_bytes=64)
         nc.vector.tensor_copy(got_scales[:], key_scales[:].indirect(offsets[:]))
+
+        got_words = sb.tile([P, I], U16, name="got_words", align_bytes=64)
+        nc.vector.tensor_copy(got_words[:], key_words[:].indirect(offsets[:]))
 
         scores = []
         for name, raw in zip(("q", "dq"), raw_q):
@@ -79,7 +82,7 @@ def tile_attend_ttmixedparts_kernel(tc, query, keys_words, keys_scales, share, d
             codes = sb.tile([P, Q], U32, name="codes_" + name, align_bytes=64)
             scales = sb.tile([P, Q], U8, name="scales_" + name, align_bytes=64)
             nc.vector.quantize_mx(out=codes[:].bitcast(FP8X4), scales=scales[:], in_=grouped[:])
-            acc = ps.tile([P, I], F32, name="score_" + name)
+            acc = ps.tile([P, I], F32, name="score_" + name, tag="bank_" + name)
             nc.tensor.matmul_mx(
                 out=acc[:], lhsT=codes[:].bitcast(FP8X4), lhsT_scale=scales[:],
                 rhs=got_words[:].bitcast(FP4X4), rhs_scale=got_scales[:], start=True, stop=True,
@@ -94,58 +97,58 @@ def tile_attend_ttmixedparts_kernel(tc, query, keys_words, keys_scales, share, d
         for t in range(PACK):
             nc.tensor.transpose(os_rows[:, t, :], os_cols[:, t : t + 1].to_broadcast([P, P]), ident[:])
 
-        def turn(src, name):
+        def turn(src, bank, place):
             words = src[:].bitcast(F32)
-            turned = ps_turn.tile([P, 2, P], F32, name="turned")
             for u in range(2):
-                nc.tensor.transpose(turned[:, u, :], words[:, u : I // 2 : 2], ident[:])
-            grouped = sb.tile([P, P * PACK], BF16, name="grouped_" + name, align_bytes=64)
+                nc.tensor.transpose(bank[:, 2 * place + u, :], words[:, u : I // 2 : 2], ident[:])
+
+        def interleave(bank, tiles, name, tag):
+            grouped = sb.tile([P, tiles * P * PACK], BF16, name=name, tag=tag, align_bytes=64)
             nc.scalar.copy(
-                grouped[:].bitcast(F32).rearrange("p (r u) -> p r u", u=2),
-                turned[:].rearrange("p u r -> p r u"),
+                grouped[:].bitcast(F32).rearrange("p (m r u) -> p m r u", m=tiles, u=2),
+                bank[:].rearrange("p (m u) r -> p m r u", u=2),
             )
             return grouped
 
-        v_codes = sb.tile([P, E], U32, name="v_codes", align_bytes=64)
-        v_scales = sb.tile([P, E], U8, name="v_scales", align_bytes=64)
+        bank_01 = ps_turn.tile([P, 4, P], F32, name="bank_01")
+        bank_2w = ps_turn.tile([P, 4, P], F32, name="bank_2w")
+        bank_3 = ps_turn.tile([P, 2, P], F32, name="bank_3")
 
         def gather_vals(j, tag):
             got = sb.tile([P, I], BF16, name="got_vals%d" % j, tag=tag, align_bytes=64)
             nc.vector.tensor_copy(got[:], pool_vals[j][:].indirect(offsets[:]))
-            return turn(got, "v%d" % j)
+            return got
 
-        def quantize_vals(j, grouped):
-            cols = slice(j * P, (j + 1) * P)
-            nc.vector.quantize_mx(out=v_codes[:, cols].bitcast(FP8X4), scales=v_scales[:, cols], in_=grouped[:])
-
-        rest = sb.tile([P, I], F32, name="rest")
+        rest = sb.tile([P, I], F32, name="rest", tag="rest", align_bytes=64)
         nc.scalar.activation(rest[:], a[:], ACT.Sigmoid, scale=-1.0)
         e0 = sb.tile([P, I], F32, name="e0")
         nc.scalar.activation(e0[:], a[:], ACT.Exp)
-        mix = sb.tile([P, I], F32, name="mix", tag="mix", align_bytes=64)
+        mix = sb.tile([P, I], F32, name="mix")
         nc.scalar.activation(mix[:], rest[:], ACT.Identity, bias=share_col[:], scale=coef[:])
-
-        g0 = gather_vals(0, "first")
+        turn(gather_vals(0, "first"), bank_01, 0)
         curv = sb.tile([P, I], F32, name="curv", tag="curv", align_bytes=64)
         nc.vector.scalar_tensor_tensor(curv[:], rest[:], coef[:], rest[:], MULT, MULT)
         slope = sb.tile([P, I], F32, name="slope")
         nc.vector.scalar_tensor_tensor(slope[:], curv[:], share_col[:], ta[:], ADD, MULT)
-        g1 = gather_vals(1, "curv")
-        tp = sb.tile([P, I], F32, name="tp")
+        turn(gather_vals(1, "second"), bank_01, 1)
+        narrow = sb.tile([P, T], BF16, name="narrow", tag="rest", align_bytes=64)
+        for cols in halves:
+            nc.scalar.activation(narrow[:, cols], pool_vals[2][:, cols], ACT.Copy)
+        got2 = sb.tile([P, I], BF16, name="got_vals2", tag="got2", align_bytes=64)
+        nc.scalar.activation(got2[:], narrow[:].indirect(offsets[:]), ACT.Copy)
+        g01 = interleave(bank_01, 2, "grouped_01", "rest")
+        both = sb.tile([P, 2 * I], F32, name="both", tag="vals1", align_bytes=64)
+        part, tp = both[:, 0:I], both[:, I : 2 * I]
         tz = sb.tile([P, 1], F32, name="tz")
-        nc.vector.scalar_tensor_tensor(tp[:], slope[:], 1.0, e0[:], MULT, MULT, accum_out=tz[:])
-        part = sb.tile([P, I], F32, name="part")
+        nc.vector.scalar_tensor_tensor(tp, slope[:], 1.0, e0[:], MULT, MULT, accum_out=tz[:])
         z = sb.tile([P, 1], F32, name="z")
-        nc.vector.scalar_tensor_tensor(part[:], mix[:], 1.0, e0[:], MULT, MULT, accum_out=z[:])
-        g2 = gather_vals(2, "mix")
+        nc.vector.scalar_tensor_tensor(part, mix[:], 1.0, e0[:], MULT, MULT, accum_out=z[:])
         rz = sb.tile([P, 1], F32, name="rz")
         nc.vector.reciprocal(rz[:], z[:])
-        quantize_vals(0, g0)
         neg_k = sb.tile([P, 1], F32, name="neg_k")
         nc.vector.tensor_scalar(neg_k[:], tz[:], rz[:], -1.0, MULT, MULT)
         centred = sb.tile([P, I], F32, name="centred", tag="centred", align_bytes=64)
-        nc.vector.scalar_tensor_tensor(centred[:], part[:], neg_k[:], tp[:], MULT, ADD)
-        quantize_vals(1, g1)
+        nc.vector.scalar_tensor_tensor(centred[:], part, neg_k[:], tp, MULT, ADD)
         w = sb.tile([P, I], BF16, name="w", align_bytes=64)
         nc.vector.scalar_tensor_tensor(
             w[:].rearrange("q (p t) -> q p t", t=PACK),
@@ -154,30 +157,39 @@ def tile_attend_ttmixedparts_kernel(tc, query, keys_words, keys_scales, share, d
             os_rows[:].rearrange("q t p -> q p t"),
             MULT, MULT,
         )
-        gw = turn(w, "w")
-        g3 = gather_vals(3, "centred")
-        quantize_vals(2, g2)
-        w_codes = sb.tile([P, Q], U32, name="w_codes", align_bytes=64)
-        w_scales = sb.tile([P, Q], U8, name="w_scales", align_bytes=64)
-        nc.vector.quantize_mx(out=w_codes[:].bitcast(FP8X4), scales=w_scales[:], in_=gw[:])
+        turn(w, bank_2w, 1)
+        turn(got2, bank_2w, 0)
+        g2w = interleave(bank_2w, 2, "grouped_2w", "grouped_2w")
+        got3 = gather_vals(3, "fourth")
+        turn(got3, bank_3, 0)
+        g3 = interleave(bank_3, 1, "grouped_3", "got2")
 
-        def product(acc, at, cols):
-            n = cols.stop - cols.start
+        codes = sb.tile([P, Q + E], U32, name="codes", tag="vals3", align_bytes=64)
+        scales = sb.tile([P, Q + E], U8, name="scales", align_bytes=64)
+
+        def quantize(grouped, first, tiles):
+            cols = slice(first * P, (first + tiles) * P)
+            nc.vector.quantize_mx(out=codes[:, cols].bitcast(FP8X4), scales=scales[:, cols], in_=grouped[:])
+
+        def product(acc, first, tiles):
+            cols = slice(first * P, (first + tiles) * P)
+            w_cols = slice(3 * P, 4 * P)
             nc.tensor.matmul_mx(
-                out=acc[:, at : at + n], lhsT=w_codes[:].bitcast(FP8X4), lhsT_scale=w_scales[:],
-                rhs=v_codes[:, cols].bitcast(FP8X4), rhs_scale=v_scales[:, cols], start=True, stop=True,
+                out=acc, lhsT=codes[:, w_cols].bitcast(FP8X4), lhsT_scale=scales[:, w_cols],
+                rhs=codes[:, cols].bitcast(FP8X4), rhs_scale=scales[:, cols], start=True, stop=True,
             )
 
-        early = ps.tile([P, 3 * P], F32, name="early")
-        product(early, 0, slice(0, 2 * P))
-        product(early, 2 * P, slice(2 * P, 3 * P))
+        quantize(g01, 0, 2)
+        quantize(g2w, 2, 2)
+        early = ps.tile([P, 3 * P], F32, name="early", tag="bank_q")
+        product(early[:, 0 : 2 * P], 0, 2)
+        product(early[:, 2 * P : 3 * P], 2, 1)
+        quantize(g3, 4, 1)
+        late = ps.tile([P, P], F32, name="late", tag="bank_dq")
+        product(late[:], 4, 1)
         early_sb = sb.tile([P, 3 * P], F32, name="early_sb")
         nc.scalar.copy(early_sb[:], early[:])
         nc.sync.dma_start(out[:, 0 : 3 * P], early_sb[:])
-
-        quantize_vals(3, g3)
-        late = ps.tile([P, P], F32, name="late")
-        product(late, 0, slice(3 * P, 4 * P))
         late_sb = sb.tile([P, P], F32, name="late_sb")
         nc.vector.tensor_copy(late_sb[:], late[:])
         nc.sync.dma_start(out[:, 3 * P : 4 * P], late_sb[:])

@@ -43,15 +43,13 @@ def tile_attend_ttmixedparts_kernel(tc, query, keys_words, keys_scales, share, d
         key_words = sb.tile([P, T], U16, name="key_words", align_bytes=64)
         nc.sync.dma_start(key_words[:].bitcast(I32), keys_words[0].bitcast(I32))
         halves = [slice(0, T // 2), slice(T // 2, T)]
-        raw_q = []
-        for name, src in (("q", query), ("dq", dquery)):
-            raw = sb.tile([P, PACK, Q], F32, name="raw_" + name)
-            nc.sync.dma_start(raw[:], src.rearrange("(p j) q -> p j q", j=PACK))
-            raw_q.append(raw)
         pool_vals = [sb.tile([P, T], F32, name="vals%d" % j, tag="vals%d" % j, align_bytes=64) for j in range(E_TILES)]
+        raw_q = [sb.tile([P, PACK, Q], F32, name="raw_" + name, tag="raw_" + name) for name in ("q", "dq")]
+        nc.sync.dma_start(raw_q[0][:], query.rearrange("(p j) q -> p j q", j=PACK))
         nc.sync.dma_start(pool_vals[0][:], vals[0:P, :])
         share_col = sb.tile([P, 1], F32, name="share_col")
         nc.sync.dma_start(share_col[:], share)
+        nc.sync.dma_start(raw_q[1][:], dquery.rearrange("(p j) q -> p j q", j=PACK))
         os_cols = sb.tile([P, PACK], F32, name="os_cols")
         nc.sync.dma_start(os_cols[:], slot_factor.rearrange("o (p t) -> (o p) t", t=PACK))
         for j in range(1, E_TILES):
@@ -72,8 +70,7 @@ def tile_attend_ttmixedparts_kernel(tc, query, keys_words, keys_scales, share, d
         got_words = sb.tile([P, I], U16, name="got_words", align_bytes=64)
         nc.vector.tensor_copy(got_words[:], key_words[:].indirect(offsets[:]))
 
-        scores = []
-        for name, raw in zip(("q", "dq"), raw_q):
+        def score(name, raw):
             grouped = sb.tile([P, Q * PACK], BF16, name="grouped_" + name, align_bytes=64)
             nc.scalar.copy(
                 grouped[:].rearrange("p (c i t) -> p c t i", i=4, t=PACK),
@@ -87,13 +84,14 @@ def tile_attend_ttmixedparts_kernel(tc, query, keys_words, keys_scales, share, d
                 out=acc[:], lhsT=codes[:].bitcast(FP8X4), lhsT_scale=scales[:],
                 rhs=got_words[:].bitcast(FP4X4), rhs_scale=got_scales[:], start=True, stop=True,
             )
-            scores.append(acc)
-        a, ta = scores
+            return acc
+
+        a = score("q", raw_q[0])
 
         coef = sb.tile([P, 1], F32, name="coef")
         nc.gpsimd.tensor_scalar(coef[:], share_col[:], -3.0, 3.0, MULT, ADD)
 
-        os_rows = ps.tile([P, PACK, P], F32, name="os_rows")
+        os_rows = ps.tile([P, PACK, P], F32, name="os_rows", tag="os_rows")
         for t in range(PACK):
             nc.tensor.transpose(os_rows[:, t, :], os_cols[:, t : t + 1].to_broadcast([P, P]), ident[:])
 
@@ -121,15 +119,14 @@ def tile_attend_ttmixedparts_kernel(tc, query, keys_words, keys_scales, share, d
 
         rest = sb.tile([P, I], F32, name="rest", tag="rest", align_bytes=64)
         nc.scalar.activation(rest[:], a[:], ACT.Sigmoid, scale=-1.0)
-        e0 = sb.tile([P, I], F32, name="e0")
+        turn(gather_vals(0, "first"), bank_01, 0)
+        curv = sb.tile([P, I], F32, name="curv")
+        nc.vector.scalar_tensor_tensor(curv[:], rest[:], coef[:], rest[:], MULT, MULT)
+        ta = score("dq", raw_q[1])
+        e0 = sb.tile([P, I], F32, name="e0", tag="raw_dq")
         nc.scalar.activation(e0[:], a[:], ACT.Exp)
         mix = sb.tile([P, I], F32, name="mix")
-        nc.scalar.activation(mix[:], rest[:], ACT.Identity, bias=share_col[:], scale=coef[:])
-        turn(gather_vals(0, "first"), bank_01, 0)
-        curv = sb.tile([P, I], F32, name="curv", tag="curv", align_bytes=64)
-        nc.vector.scalar_tensor_tensor(curv[:], rest[:], coef[:], rest[:], MULT, MULT)
-        slope = sb.tile([P, I], F32, name="slope")
-        nc.vector.scalar_tensor_tensor(slope[:], curv[:], share_col[:], ta[:], ADD, MULT)
+        nc.vector.tensor_scalar(mix[:], rest[:], coef[:], share_col[:], MULT, ADD)
         turn(gather_vals(1, "second"), bank_01, 1)
         narrow = sb.tile([P, T], BF16, name="narrow", tag="rest", align_bytes=64)
         for cols in halves:
@@ -137,26 +134,30 @@ def tile_attend_ttmixedparts_kernel(tc, query, keys_words, keys_scales, share, d
         got2 = sb.tile([P, I], BF16, name="got_vals2", tag="got2", align_bytes=64)
         nc.scalar.activation(got2[:], narrow[:].indirect(offsets[:]), ACT.Copy)
         g01 = interleave(bank_01, 2, "grouped_01", "rest")
-        both = sb.tile([P, 2 * I], F32, name="both", tag="vals1", align_bytes=64)
-        part, tp = both[:, 0:I], both[:, I : 2 * I]
-        tz = sb.tile([P, 1], F32, name="tz")
-        nc.vector.scalar_tensor_tensor(tp, slope[:], 1.0, e0[:], MULT, MULT, accum_out=tz[:])
+        both = sb.tile([P, 3 * I], F32, name="both", tag="vals1", align_bytes=64)
+        part, tp, slope = both[:, 0:I], both[:, I : 2 * I], both[:, 2 * I : 3 * I]
+        nc.vector.scalar_tensor_tensor(slope, curv[:], share_col[:], ta[:], ADD, MULT)
         z = sb.tile([P, 1], F32, name="z")
         nc.vector.scalar_tensor_tensor(part, mix[:], 1.0, e0[:], MULT, MULT, accum_out=z[:])
+        tz = sb.tile([P, 1], F32, name="tz")
+        nc.vector.scalar_tensor_tensor(tp, slope, 1.0, e0[:], MULT, MULT, accum_out=tz[:])
         rz = sb.tile([P, 1], F32, name="rz")
         nc.vector.reciprocal(rz[:], z[:])
         neg_k = sb.tile([P, 1], F32, name="neg_k")
         nc.vector.tensor_scalar(neg_k[:], tz[:], rz[:], -1.0, MULT, MULT)
-        centred = sb.tile([P, I], F32, name="centred", tag="centred", align_bytes=64)
-        nc.vector.scalar_tensor_tensor(centred[:], part, neg_k[:], tp, MULT, ADD)
+        centred = sb.tile([P, I], F32, name="centred")
         w = sb.tile([P, I], BF16, name="w", align_bytes=64)
-        nc.vector.scalar_tensor_tensor(
-            w[:].rearrange("q (p t) -> q p t", t=PACK),
-            centred[:].rearrange("q (p t) -> q p t", t=PACK),
-            rz[:],
-            os_rows[:].rearrange("q t p -> q p t"),
-            MULT, MULT,
-        )
+        slot_halves = [slice(0, I // 2), slice(I // 2, I)]
+        for cols in slot_halves:
+            nc.vector.scalar_tensor_tensor(centred[:, cols], part[:, cols], neg_k[:], tp[:, cols], MULT, ADD)
+        for cols in slot_halves:
+            nc.vector.scalar_tensor_tensor(
+                w[:, cols].rearrange("q (p t) -> q p t", t=PACK),
+                centred[:, cols].rearrange("q (p t) -> q p t", t=PACK),
+                rz[:],
+                os_rows[:, :, cols.start // PACK : cols.stop // PACK].rearrange("q t p -> q p t"),
+                MULT, MULT,
+            )
         turn(w, bank_2w, 1)
         turn(got2, bank_2w, 0)
         g2w = interleave(bank_2w, 2, "grouped_2w", "grouped_2w")
@@ -181,15 +182,17 @@ def tile_attend_ttmixedparts_kernel(tc, query, keys_words, keys_scales, share, d
 
         quantize(g01, 0, 2)
         quantize(g2w, 2, 2)
-        early = ps.tile([P, 3 * P], F32, name="early", tag="bank_q")
-        product(early[:, 0 : 2 * P], 0, 2)
-        product(early[:, 2 * P : 3 * P], 2, 1)
+        low = ps.tile([P, 2 * P], F32, name="low", tag="bank_q")
+        product(low[:], 0, 2)
+        third = ps.tile([P, P], F32, name="third", tag="bank_dq")
+        product(third[:], 2, 1)
         quantize(g3, 4, 1)
-        late = ps.tile([P, P], F32, name="late", tag="bank_dq")
-        product(late[:], 4, 1)
-        early_sb = sb.tile([P, 3 * P], F32, name="early_sb")
-        nc.scalar.copy(early_sb[:], early[:])
-        nc.sync.dma_start(out[:, 0 : 3 * P], early_sb[:])
-        late_sb = sb.tile([P, P], F32, name="late_sb")
-        nc.vector.tensor_copy(late_sb[:], late[:])
-        nc.sync.dma_start(out[:, 3 * P : 4 * P], late_sb[:])
+        fourth = ps.tile([P, P], F32, name="fourth", tag="os_rows")
+        product(fourth[:], 4, 1)
+        low_sb = sb.tile([P, 2 * P], F32, name="low_sb")
+        nc.scalar.copy(low_sb[:], low[:])
+        nc.scalar.dma_start(out[:, 0 : 2 * P], low_sb[:])
+        high_sb = sb.tile([P, 2 * P], F32, name="high_sb")
+        nc.vector.tensor_copy(high_sb[:, 0:P], third[:])
+        nc.vector.tensor_copy(high_sb[:, P : 2 * P], fourth[:])
+        nc.sync.dma_start(out[:, 2 * P : 4 * P], high_sb[:])

@@ -46,10 +46,10 @@ def tile_attend_ttmixedparts_kernel(tc, query, keys_words, keys_scales, share, d
         pool_vals = [sb.tile([P, T], F32, name="vals%d" % j, tag="vals%d" % j, align_bytes=64) for j in range(E_TILES)]
         raw_q = [sb.tile([P, PACK, Q], F32, name="raw_" + name, tag="raw_" + name) for name in ("q", "dq")]
         nc.sync.dma_start(raw_q[0][:], query.rearrange("(p j) q -> p j q", j=PACK))
+        nc.sync.dma_start(raw_q[1][:], dquery.rearrange("(p j) q -> p j q", j=PACK))
         nc.sync.dma_start(pool_vals[0][:], vals[0:P, :])
         share_col = sb.tile([P, 1], F32, name="share_col")
         nc.sync.dma_start(share_col[:], share)
-        nc.sync.dma_start(raw_q[1][:], dquery.rearrange("(p j) q -> p j q", j=PACK))
         os_cols = sb.tile([P, PACK], F32, name="os_cols")
         nc.sync.dma_start(os_cols[:], slot_factor.rearrange("o (p t) -> (o p) t", t=PACK))
         for j in range(1, E_TILES):
@@ -87,6 +87,7 @@ def tile_attend_ttmixedparts_kernel(tc, query, keys_words, keys_scales, share, d
             return acc
 
         a = score("q", raw_q[0])
+        ta = score("dq", raw_q[1])
 
         coef = sb.tile([P, 1], F32, name="coef")
         nc.gpsimd.tensor_scalar(coef[:], share_col[:], -3.0, 3.0, MULT, ADD)
@@ -108,7 +109,8 @@ def tile_attend_ttmixedparts_kernel(tc, query, keys_words, keys_scales, share, d
             )
             return grouped
 
-        bank_01 = ps_turn.tile([P, 4, P], F32, name="bank_01")
+        bank_0 = ps_turn.tile([P, 2, P], F32, name="bank_0")
+        bank_1 = ps_turn.tile([P, 2, P], F32, name="bank_1")
         bank_2w = ps_turn.tile([P, 4, P], F32, name="bank_2w")
         bank_3 = ps_turn.tile([P, 2, P], F32, name="bank_3")
 
@@ -119,28 +121,29 @@ def tile_attend_ttmixedparts_kernel(tc, query, keys_words, keys_scales, share, d
 
         rest = sb.tile([P, I], F32, name="rest", tag="rest", align_bytes=64)
         nc.scalar.activation(rest[:], a[:], ACT.Sigmoid, scale=-1.0)
-        turn(gather_vals(0, "first"), bank_01, 0)
+        e0 = sb.tile([P, I], F32, name="e0")
+        nc.scalar.activation(e0[:], a[:], ACT.Exp)
+        turn(gather_vals(0, "first"), bank_0, 0)
+        g0 = interleave(bank_0, 1, "grouped_0", "grouped_0")
         curv = sb.tile([P, I], F32, name="curv")
         nc.vector.scalar_tensor_tensor(curv[:], rest[:], coef[:], rest[:], MULT, MULT)
-        ta = score("dq", raw_q[1])
-        e0 = sb.tile([P, I], F32, name="e0", tag="raw_dq")
-        nc.scalar.activation(e0[:], a[:], ACT.Exp)
         mix = sb.tile([P, I], F32, name="mix")
         nc.vector.tensor_scalar(mix[:], rest[:], coef[:], share_col[:], MULT, ADD)
-        turn(gather_vals(1, "second"), bank_01, 1)
+        slope = sb.tile([P, I], F32, name="slope")
+        nc.vector.scalar_tensor_tensor(slope[:], curv[:], share_col[:], ta[:], ADD, MULT)
+        turn(gather_vals(1, "second"), bank_1, 0)
         narrow = sb.tile([P, T], BF16, name="narrow", tag="rest", align_bytes=64)
         for cols in halves:
             nc.scalar.activation(narrow[:, cols], pool_vals[2][:, cols], ACT.Copy)
         got2 = sb.tile([P, I], BF16, name="got_vals2", tag="got2", align_bytes=64)
         nc.scalar.activation(got2[:], narrow[:].indirect(offsets[:]), ACT.Copy)
-        g01 = interleave(bank_01, 2, "grouped_01", "rest")
-        both = sb.tile([P, 3 * I], F32, name="both", tag="vals1", align_bytes=64)
-        part, tp, slope = both[:, 0:I], both[:, I : 2 * I], both[:, 2 * I : 3 * I]
-        nc.vector.scalar_tensor_tensor(slope, curv[:], share_col[:], ta[:], ADD, MULT)
+        g1 = interleave(bank_1, 1, "grouped_1", "rest")
+        both = sb.tile([P, 2 * I], F32, name="both", tag="vals1", align_bytes=64)
+        part, tp = both[:, 0:I], both[:, I : 2 * I]
         z = sb.tile([P, 1], F32, name="z")
         nc.vector.scalar_tensor_tensor(part, mix[:], 1.0, e0[:], MULT, MULT, accum_out=z[:])
         tz = sb.tile([P, 1], F32, name="tz")
-        nc.vector.scalar_tensor_tensor(tp, slope, 1.0, e0[:], MULT, MULT, accum_out=tz[:])
+        nc.vector.scalar_tensor_tensor(tp, slope[:], 1.0, e0[:], MULT, MULT, accum_out=tz[:])
         rz = sb.tile([P, 1], F32, name="rz")
         nc.vector.reciprocal(rz[:], z[:])
         neg_k = sb.tile([P, 1], F32, name="neg_k")
@@ -180,7 +183,8 @@ def tile_attend_ttmixedparts_kernel(tc, query, keys_words, keys_scales, share, d
                 rhs=codes[:, cols].bitcast(FP8X4), rhs_scale=scales[:, cols], start=True, stop=True,
             )
 
-        quantize(g01, 0, 2)
+        quantize(g0, 0, 1)
+        quantize(g1, 1, 1)
         quantize(g2w, 2, 2)
         low = ps.tile([P, 2 * P], F32, name="low", tag="bank_q")
         product(low[:], 0, 2)
@@ -192,7 +196,7 @@ def tile_attend_ttmixedparts_kernel(tc, query, keys_words, keys_scales, share, d
         low_sb = sb.tile([P, 2 * P], F32, name="low_sb")
         nc.scalar.copy(low_sb[:], low[:])
         nc.scalar.dma_start(out[:, 0 : 2 * P], low_sb[:])
-        high_sb = sb.tile([P, 2 * P], F32, name="high_sb")
-        nc.vector.tensor_copy(high_sb[:, 0:P], third[:])
-        nc.vector.tensor_copy(high_sb[:, P : 2 * P], fourth[:])
-        nc.sync.dma_start(out[:, 2 * P : 4 * P], high_sb[:])
+        for j, acc in ((2, third), (3, fourth)):
+            done = sb.tile([P, P], F32, name="done%d" % j)
+            nc.vector.tensor_copy(done[:], acc[:])
+            nc.sync.dma_start(out[:, j * P : (j + 1) * P], done[:])

from contextlib import ExitStack

import concourse.mybir as mybir
from concourse.masks import make_identity

D, E, T, I, Q = 512, 512, 2048, 512, 128
FLOPS = 2 * (2 * Q * D * I + Q * I * E)

F32 = mybir.dt.float32
BF16 = mybir.dt.bfloat16
I32 = mybir.dt.int32
U32 = mybir.dt.uint32
U16 = mybir.dt.uint16
U8 = mybir.dt.uint8
FP8X4 = mybir.dt.float8_e4m3fn_x4
FP4X4 = mybir.dt.float4_e2m1fn_x4
ACT = mybir.ActivationFunctionType
MULT = mybir.AluOpType.mult
ADD = mybir.AluOpType.add

P = 128
PACK = 4
E_TILES = E // P


def tile_attend_ttmixedparts_kernel(tc, query, keys_words, keys_scales, share, dquery, slot_factor, vals, offs, out):
    nc = tc.nc
    with ExitStack() as ctx:
        sb = ctx.enter_context(tc.tile_pool(name="sb", bufs=1))
        ps = ctx.enter_context(tc.psum_pool(name="ps", bufs=1))
        ps_turn = ctx.enter_context(tc.psum_pool(name="ps_turn", bufs=1))

        offsets = sb.tile([P, I // 16], U16, name="offsets")
        nc.sync.dma_start(offsets[:], offs)

        key_scales = sb.tile([P, T], U8, name="key_scales", align_bytes=64)
        nc.gpsimd.memset(key_scales[:].bitcast(I32), 0)
        for quad in range(4):
            nc.sync.dma_start(
                key_scales[32 * quad : 32 * quad + 4, :].bitcast(I32),
                keys_scales[0, 4 * quad : 4 * quad + 4, :].bitcast(I32),
            )
        key_words = sb.tile([P, T], U16, name="key_words", align_bytes=64)
        nc.sync.dma_start(key_words[:].bitcast(I32), keys_words[0].bitcast(I32))
        halves = [slice(0, T // 2), slice(T // 2, T)]
        pool_vals = [sb.tile([P, T], F32, name="vals%d" % j, tag="vals%d" % j, align_bytes=64) for j in range(E_TILES)]
        raw_q = [sb.tile([P, PACK, Q], F32, name="raw_" + name, tag="raw_" + name) for name in ("q", "dq")]
        nc.sync.dma_start(raw_q[0][:], query.rearrange("(p j) q -> p j q", j=PACK))
        nc.sync.dma_start(raw_q[1][:], dquery.rearrange("(p j) q -> p j q", j=PACK))
        nc.sync.dma_start(pool_vals[0][:], vals[0:P, :])
        share_col = sb.tile([P, 1], F32, name="share_col")
        nc.sync.dma_start(share_col[:], share)
        os_cols = sb.tile([P, PACK], F32, name="os_cols")
        nc.sync.dma_start(os_cols[:], slot_factor.rearrange("o (p t) -> (o p) t", t=PACK))
        for j in range(1, E_TILES):
            for cols in (halves if j == 2 else [slice(0, T)]):
                nc.sync.dma_start(pool_vals[j][:, cols], vals[j * P : (j + 1) * P, cols])

        warm = sb.tile([P, 1], F32, name="warm")
        nc.gpsimd.memset(warm[:], 0.0)
        warm_out = sb.tile([P, 1], F32, name="warm_out")
        nc.scalar.activation(warm_out[:], warm[:], ACT.Sigmoid)

        ident = sb.tile([P, P], F32, name="ident")
        make_identity(nc, ident[:])

        got_scales = sb.tile([P, I], U8, name="got_scales", align_bytes=64)
        nc.vector.tensor_copy(got_scales[:], key_scales[:].indirect(offsets[:]))

        got_words = sb.tile([P, I], U16, name="got_words", align_bytes=64)
        nc.vector.tensor_copy(got_words[:], key_words[:].indirect(offsets[:]))

        def score(name, raw):
            grouped = sb.tile([P, Q * PACK], BF16, name="grouped_" + name, align_bytes=64)
            nc.scalar.copy(
                grouped[:].rearrange("p (c i t) -> p c t i", i=4, t=PACK),
                raw[:].rearrange("p t (c i) -> p c t i", i=4),
            )
            codes = sb.tile([P, Q], U32, name="codes_" + name, align_bytes=64)
            scales = sb.tile([P, Q], U8, name="scales_" + name, align_bytes=64)
            nc.vector.quantize_mx(out=codes[:].bitcast(FP8X4), scales=scales[:], in_=grouped[:])
            acc = ps.tile([P, I], F32, name="score_" + name, tag="bank_" + name)
            nc.tensor.matmul_mx(
                out=acc[:], lhsT=codes[:].bitcast(FP8X4), lhsT_scale=scales[:],
                rhs=got_words[:].bitcast(FP4X4), rhs_scale=got_scales[:], start=True, stop=True,
            )
            return acc

        a = score("q", raw_q[0])
        ta = score("dq", raw_q[1])

        coef = sb.tile([P, 1], F32, name="coef")
        nc.gpsimd.tensor_scalar(coef[:], share_col[:], -3.0, 3.0, MULT, ADD)

        os_rows = ps.tile([P, PACK, P], F32, name="os_rows", tag="os_rows")
        for t in range(PACK):
            nc.tensor.transpose(os_rows[:, t, :], os_cols[:, t : t + 1].to_broadcast([P, P]), ident[:])

        def turn(src, bank, place):
            words = src[:].bitcast(F32)
            for u in range(2):
                nc.tensor.transpose(bank[:, 2 * place + u, :], words[:, u : I // 2 : 2], ident[:])

        def interleave(bank, tiles, name, tag):
            grouped = sb.tile([P, tiles * P * PACK], BF16, name=name, tag=tag, align_bytes=64)
            nc.scalar.copy(
                grouped[:].bitcast(F32).rearrange("p (m r u) -> p m r u", m=tiles, u=2),
                bank[:].rearrange("p (m u) r -> p m r u", u=2),
            )
            return grouped

        bank_0 = ps_turn.tile([P, 2, P], F32, name="bank_0")
        bank_1 = ps_turn.tile([P, 2, P], F32, name="bank_1")
        bank_2w = ps_turn.tile([P, 4, P], F32, name="bank_2w")
        bank_3 = ps_turn.tile([P, 2, P], F32, name="bank_3")

        def gather_vals(j, tag):
            got = sb.tile([P, I], BF16, name="got_vals%d" % j, tag=tag, align_bytes=64)
            nc.vector.tensor_copy(got[:], pool_vals[j][:].indirect(offsets[:]))
            return got

        rest = sb.tile([P, I], F32, name="rest", tag="rest", align_bytes=64)
        nc.scalar.activation(rest[:], a[:], ACT.Sigmoid, scale=-1.0)
        e0 = sb.tile([P, I], F32, name="e0")
        nc.scalar.activation(e0[:], a[:], ACT.Exp)
        turn(gather_vals(0, "first"), bank_0, 0)
        g0 = interleave(bank_0, 1, "grouped_0", "grouped_0")
        curv = sb.tile([P, I], F32, name="curv")
        nc.vector.scalar_tensor_tensor(curv[:], rest[:], coef[:], rest[:], MULT, MULT)
        mix = sb.tile([P, I], F32, name="mix")
        nc.vector.tensor_scalar(mix[:], rest[:], coef[:], share_col[:], MULT, ADD)
        slope = sb.tile([P, I], F32, name="slope")
        nc.vector.scalar_tensor_tensor(slope[:], curv[:], share_col[:], ta[:], ADD, MULT)
        turn(gather_vals(1, "second"), bank_1, 0)
        narrow = sb.tile([P, T], BF16, name="narrow", tag="rest", align_bytes=64)
        for cols in halves:
            nc.scalar.activation(narrow[:, cols], pool_vals[2][:, cols], ACT.Copy)
        got2 = sb.tile([P, I], BF16, name="got_vals2", tag="got2", align_bytes=64)
        nc.scalar.activation(got2[:], narrow[:].indirect(offsets[:]), ACT.Copy)
        g1 = interleave(bank_1, 1, "grouped_1", "rest")
        both = sb.tile([P, 2 * I], F32, name="both", tag="vals1", align_bytes=64)
        part, tp = both[:, 0:I], both[:, I : 2 * I]
        z = sb.tile([P, 1], F32, name="z")
        nc.vector.scalar_tensor_tensor(part, mix[:], 1.0, e0[:], MULT, MULT, accum_out=z[:])
        tz = sb.tile([P, 1], F32, name="tz")
        nc.vector.scalar_tensor_tensor(tp, slope[:], 1.0, e0[:], MULT, MULT, accum_out=tz[:])
        rz = sb.tile([P, 1], F32, name="rz")
        nc.vector.reciprocal(rz[:], z[:])
        neg_k = sb.tile([P, 1], F32, name="neg_k")
        nc.vector.tensor_scalar(neg_k[:], tz[:], rz[:], -1.0, MULT, MULT)
        centred = sb.tile([P, I], F32, name="centred")
        w = sb.tile([P, I], BF16, name="w", align_bytes=64)
        slot_halves = [slice(0, I // 2), slice(I // 2, I)]
        for cols in slot_halves:
            nc.vector.scalar_tensor_tensor(centred[:, cols], part[:, cols], neg_k[:], tp[:, cols], MULT, ADD)
        for cols in slot_halves:
            nc.vector.scalar_tensor_tensor(
                w[:, cols].rearrange("q (p t) -> q p t", t=PACK),
                centred[:, cols].rearrange("q (p t) -> q p t", t=PACK),
                rz[:],
                os_rows[:, :, cols.start // PACK : cols.stop // PACK].rearrange("q t p -> q p t"),
                MULT, MULT,
            )
        turn(w, bank_2w, 1)
        turn(got2, bank_2w, 0)
        g2w = interleave(bank_2w, 2, "grouped_2w", "grouped_2w")
        got3 = gather_vals(3, "fourth")
        turn(got3, bank_3, 0)
        g3 = interleave(bank_3, 1, "grouped_3", "got2")

        codes = sb.tile([P, Q + E], U32, name="codes", tag="vals3", align_bytes=64)
        scales = sb.tile([P, Q + E], U8, name="scales", align_bytes=64)

        def quantize(grouped, first, tiles):
            cols = slice(first * P, (first + tiles) * P)
            nc.vector.quantize_mx(out=codes[:, cols].bitcast(FP8X4), scales=scales[:, cols], in_=grouped[:])

        def product(acc, first, tiles):
            cols = slice(first * P, (first + tiles) * P)
            w_cols = slice(3 * P, 4 * P)
            nc.tensor.matmul_mx(
                out=acc, lhsT=codes[:, w_cols].bitcast(FP8X4), lhsT_scale=scales[:, w_cols],
                rhs=codes[:, cols].bitcast(FP8X4), rhs_scale=scales[:, cols], start=True, stop=True,
            )

        quantize(g0, 0, 1)
        quantize(g1, 1, 1)
        quantize(g2w, 2, 2)
        low = ps.tile([P, 2 * P], F32, name="low", tag="bank_q")
        product(low[:], 0, 2)
        third = ps.tile([P, P], F32, name="third", tag="bank_dq")
        product(third[:], 2, 1)
        quantize(g3, 4, 1)
        fourth = ps.tile([P, P], F32, name="fourth", tag="os_rows")
        product(fourth[:], 4, 1)
        low_sb = sb.tile([P, 2 * P], F32, name="low_sb")
        nc.scalar.copy(low_sb[:], low[:])
        nc.scalar.dma_start(out[:, 0 : 2 * P], low_sb[:])
        for j, acc in ((2, third), (3, fourth)):
            done = sb.tile([P, P], F32, name="done%d" % j)
            nc.vector.tensor_copy(done[:], acc[:])
            nc.sync.dma_start(out[:, j * P : (j + 1) * P], done[:])
